import numpy as np
import ml_dtypes


def mxq(x, axis, fmt="e4m3"):
    dtype, down = {"e4m3": (ml_dtypes.float8_e4m3fn, 7), "e5m2": (ml_dtypes.float8_e5m2, 14)}[fmt]
    v = np.moveaxis(np.asarray(x, np.float32).astype(ml_dtypes.bfloat16).astype(np.float64), axis, -1)
    blocks = v.reshape(v.shape[:-1] + (-1, 32))
    amax = np.abs(blocks).max(-1, keepdims=True)
    byte = np.maximum(np.where(amax > 0, np.frexp(amax)[1] - 1 + 127, 0) - down, 1)
    scale = np.exp2(byte - 127.0)
    codes = (blocks / scale).astype(np.float32).astype(dtype).astype(np.float64)
    return np.moveaxis((codes * scale).reshape(v.shape), -1, axis)


WIDE = False


def mx_kscale(k):
    if not WIDE:
        return np.ones(k)
    levels = np.array([30, -30])
    if k % 512:
        return np.exp2(np.random.permutation(np.resize(levels, k // 32))).repeat(32)
    a = np.empty((k // 512, 16))
    for p in range(k // 512):
        a[p, :8] = np.random.permutation(np.resize(levels, 8))
        for g in range(8):
            far = levels[np.abs(levels - a[p, g]) >= 10]
            a[p, g + 8] = far[np.random.randint(len(far))]
    return np.exp2(a.ravel()).repeat(32)


BF16 = ml_dtypes.bfloat16


def bf(x):
    return np.asarray(x, np.float32).astype(BF16)


def f64(x):
    return np.asarray(x).astype(np.float64)


E2M1 = np.array([0.0, 0.5, 1.0, 1.5, 2.0, 3.0, 4.0, 6.0, -0.0, -0.5, -1.0, -1.5, -2.0, -3.0, -4.0, -6.0])


def pack_weight(w, fmt):
    k, n = w.shape
    w = f64(bf(w)).reshape(k // 32, 32, n)
    amax = np.abs(w).max(1)
    if fmt in ("e4m3", "e5m2"):
        byte = np.frexp(amax)[1] - 1 + 127 - (7 if fmt == "e4m3" else 14)
    else:
        mant, ex = np.frexp(amax / 6.0)
        byte = np.where(mant > 0.5, ex, ex - 1) + 127
    byte = np.clip(np.where(amax > 0, byte, 1), 1, 254)
    scaled = (w * np.exp2(127.0 - byte)[:, None, :]).reshape(k, n).astype(np.float32)
    by_word = np.ascontiguousarray(scaled.reshape(k // 512, 128, 4, n).transpose(0, 1, 3, 2))
    if fmt in ("e4m3", "e5m2"):
        words = by_word.astype(ml_dtypes.float8_e4m3fn if fmt == "e4m3" else ml_dtypes.float8_e5m2).view(np.uint8)
    else:
        c = by_word.astype(ml_dtypes.float4_e2m1fn).view(np.uint8) & 0xF
        words = c[..., 0::2] | (c[..., 1::2] << 4)
    return np.ascontiguousarray(words), np.ascontiguousarray(byte.astype(np.uint8).reshape(k // 512, 16, n))


def unpack_weight(words, scales, fmt):
    g, p, n, _ = words.shape
    if fmt in ("e4m3", "e5m2"):
        vals = np.ascontiguousarray(words).view(ml_dtypes.float8_e4m3fn if fmt == "e4m3" else ml_dtypes.float8_e5m2).astype(np.float64)
    else:
        nib = np.empty((g, p, n, 4), np.uint8)
        nib[..., 0::2] = words & 0xF
        nib[..., 1::2] = words >> 4
        vals = E2M1[nib]
    vals = vals * np.repeat(np.exp2(scales.astype(np.float64) - 127.0), 8, axis=1)[..., None]
    return vals.transpose(0, 1, 3, 2).reshape(g * 512, n)


T, L, C, B = 1152, 1536, 512, 2048


def setup_inputs():
    s = mx_kscale(L)
    u = mx_kscale(C)
    G = np.random.standard_t(4, (L, T)) / np.sqrt(2.0) * s[:, None]
    shadow_words, shadow_scales = pack_weight(G, "e5m2")
    return {"shadow_words": shadow_words,
            "shadow_scales": shadow_scales,
            "ptdf": bf(np.random.standard_normal((L, B)) / np.sqrt(L) / s[:, None]),
            "cshadow": bf(np.random.standard_normal((T, C)) * u),
            "otdf": bf(np.random.standard_normal((C, B)) / np.sqrt(C) / u[:, None]),
            "energy": bf(1.0 + 0.5 * np.random.standard_normal(T)),
            "delivery": bf(1.0 + 0.1 * np.random.standard_normal(B))}


def reference(shadow_words, shadow_scales, ptdf, cshadow, otdf, energy, delivery):
    G = unpack_weight(shadow_words, shadow_scales, "e5m2")
    base = G.T @ mxq(f64(ptdf), 0, "e4m3")
    cont = mxq(f64(cshadow), 1, "e4m3") @ mxq(f64(otdf), 0, "e4m3")
    return f64(energy)[:, None] * f64(delivery)[None, :] - (base + cont)

@@ -1,0 +1,258 @@
+from contextlib import ExitStack
+
+import concourse.mybir as mybir
+from concourse.masks import make_identity
+
+T, L, C, B = 1152, 1536, 512, 2048
+FLOPS = 2 * T * B * (L + C)
+
+F32 = mybir.dt.float32
+BF16 = mybir.dt.bfloat16
+U32 = mybir.dt.uint32
+I32 = mybir.dt.int32
+U8 = mybir.dt.uint8
+E4M3 = mybir.dt.float8_e4m3fn_x4
+E5M2 = mybir.dt.float8_e5m2_x4
+MULT = mybir.AluOpType.mult
+SUB = mybir.AluOpType.subtract
+
+P = 128
+NB = 512
+NI = T // P
+NG = L // 512
+NBLK = B // NB
+COLS_F = 288
+COLS_V0 = 192
+COLS_V1 = 288
+COLS_V = 64
+
+
+def tile_congested_nodal_prices_e4_kernel(
+    tc, shadow_words, shadow_scales, ptdf, cshadow, otdf, energy, delivery, out
+):
+    nc = tc.nc
+    with ExitStack() as ctx:
+        keep = ctx.enter_context(tc.tile_pool(name="keep", bufs=1))
+        work = ctx.enter_context(tc.tile_pool(name="work", bufs=4))
+        res = ctx.enter_context(tc.tile_pool(name="res", bufs=9))
+        psum = ctx.enter_context(tc.psum_pool(name="psum", bufs=8))
+
+        vec = keep.tile([P, P], BF16, name="vec", align_bytes=64)
+        vec_t = keep.tile([P, P], BF16, name="vec_t", align_bytes=64)
+        ident_b = keep.tile([P, P], BF16, name="ident_b", align_bytes=64)
+        ident_f = keep.tile([P, P], F32, name="ident_f", align_bytes=64)
+        d_bc = keep.tile([P, B], BF16, name="d_bc", align_bytes=64)
+        g_scales = keep.tile([P, NG, T], U8, name="g_scales", align_bytes=64)
+        g_words = [keep.tile([P, T], U32, name="g_words%d" % g, align_bytes=64) for g in range(NG)]
+        cs_raw = [keep.tile([P, n, C], BF16, name="cs_raw%d" % a, align_bytes=64) for a, n in enumerate((4, 5))]
+        cs_split = keep.tile([P, NI, 2, P], F32, name="cs_split", align_bytes=64)
+        cs_grp = keep.tile([P, T, 4], BF16, name="cs_grp", align_bytes=64)
+        cs_codes = keep.tile([P, T], U32, name="cs_codes", align_bytes=64)
+        cs_scales = keep.tile([P, T], U8, name="cs_scales", align_bytes=64)
+        raw = {}
+        for b, n in ((0, 512), (1, 512), (2, 1024)):
+            for k in range(4):
+                raw[k, b] = keep.tile([P, 4, n], BF16, name="raw%d_%d" % (k, b), align_bytes=64)
+        codes = {}
+        scales = {}
+        for b in range(NBLK):
+            for k in range(4):
+                codes[k, b] = keep.tile([P, NB], U32, name="codes%d_%d" % (k, b), align_bytes=64)
+                scales[k, b] = keep.tile([P, NB], U8, name="scales%d_%d" % (k, b), align_bytes=64)
+
+        ctx.enter_context(tc.manual_schedule())
+
+        nc.vector.memset(vec[:], 0.0)
+        nc.vector.memset(g_scales[:].rearrange("p g n -> p (g n)").bitcast(I32), 0)
+        make_identity(nc, ident_b[:])
+        make_identity(nc, ident_f[:])
+        nc.scalar.dma_start(out=vec[0:16, :], in_=delivery.rearrange("(c p) -> c p", p=P))
+        nc.scalar.dma_start(out=vec[16:25, :], in_=energy.rearrange("(c p) -> c p", p=P))
+        for r in range(4):
+            nc.scalar.dma_start(
+                out=g_scales[r:P:32, :, :].bitcast(I32),
+                in_=shadow_scales.rearrange("g (q r) n -> r q g n", r=4)[r].bitcast(I32),
+            )
+
+        def load_rows(k, b):
+            src = otdf if k == 3 else ptdf[512 * k : 512 * (k + 1), :]
+            c0, n = ((0, 512), (512, 512), (1024, 1024))[b]
+            nc.sync.dma_start(out=raw[k, b][:], in_=src.rearrange("(p j) b -> p j b", j=4)[:, :, c0 : c0 + n])
+
+        def load_g(g):
+            nc.sync.dma_start(
+                out=g_words[g][:].bitcast(I32),
+                in_=shadow_words[g].rearrange("p n t -> p (n t)").bitcast(I32),
+            )
+
+        cs_rows = cshadow.rearrange("(i p) c -> p i c", p=P)
+        load_rows(0, 0)
+        nc.sync.dma_start(out=cs_raw[0][:], in_=cs_rows[:, 0:4, :])
+        nc.sync.dma_start(out=cs_raw[1][:], in_=cs_rows[:, 4:9, :])
+        load_g(0)
+        for g in (1, 2):
+            load_rows(g, 0)
+            load_g(g)
+        load_rows(3, 0)
+        for b in (1, 2):
+            for k in range(4):
+                load_rows(k, b)
+
+        grp = {}
+
+        def inter(k, b, v):
+            tile = work.tile([P, NB, 4], BF16, name="grouped", align_bytes=64)
+            grp[k, b] = tile
+            src = raw[k, min(b, 2)]
+            c0 = NB if b == 3 else 0
+
+            def part(copy, lo, hi):
+                copy(
+                    out=tile[:, lo:hi, :],
+                    in_=src[:, :, c0 + lo : c0 + hi].rearrange("p j n -> p n j"),
+                )
+
+            if v > 0:
+                part(nc.vector.tensor_copy, 0, v)
+            part(nc.scalar.copy, v, NB)
+
+        def quant(k, b):
+            nc.vector.quantize_mx(
+                out=codes[k, b][:].bitcast(E4M3),
+                scales=scales[k, b][:],
+                in_=grp[k, b][:].rearrange("p n j -> p (n j)"),
+            )
+
+        acc = {}
+
+        def mm(i, b, k, start, stop):
+            if start:
+                bank = psum.tile([P, NB], F32, name="bank")
+                acc[i, b] = bank
+            cols = slice(P * i, P * (i + 1))
+            if k == 3:
+                lhs = cs_codes[:, cols].bitcast(E4M3)
+                lhs_s = cs_scales[:, cols]
+            else:
+                lhs = g_words[k][:, cols].bitcast(E5M2)
+                lhs_s = g_scales[:, k, cols]
+            nc.tensor.matmul_mx(
+                out=acc[i, b][:], lhsT=lhs, lhsT_scale=lhs_s,
+                rhs=codes[k, b][:].bitcast(E4M3), rhs_scale=scales[k, b][:],
+                start=start, stop=stop,
+            )
+
+        pair = {}
+
+        def epi(i, b):
+            cols = slice(NB * b, NB * (b + 1))
+            if b < 2:
+                if b == 0:
+                    double = res.tile([P, 2 * NB], F32, name="double", align_bytes=64)
+                    pair[i] = double
+                dst = pair[i][:, NB * b : NB * (b + 1)]
+            else:
+                single = res.tile([P, NB], F32, name="single", align_bytes=64)
+                dst = single[:]
+            nc.vector.scalar_tensor_tensor(
+                out=dst, in0=d_bc[:, cols], scalar=vec_t[:, 16 + i : 17 + i],
+                in1=acc[i, b][:], op0=MULT, op1=SUB,
+            )
+            rows = slice(P * i, P * (i + 1))
+            if b == 1:
+                nc.sync.dma_start(out=out[rows, 0 : 2 * NB], in_=pair[i][:])
+            if b > 1:
+                nc.sync.dma_start(out=out[rows, cols], in_=dst)
+
+        bank = psum.tile([P, P], BF16, name="bank")
+        nc.tensor.transpose(bank[:], vec[:], ident_b[:])
+        nc.vector.tensor_copy(out=vec_t[:], in_=bank[:])
+        inter(0, 0, COLS_F)
+        for h in range(2):
+            bank = psum.tile([P, 8, P], BF16, name="bank")
+            for c in range(8):
+                col = vec_t[:, 8 * h + c : 8 * h + c + 1]
+                nc.tensor.transpose(bank[:, c, :], col.to_broadcast([P, P]), ident_b[:])
+            nc.scalar.copy(out=d_bc[:, 1024 * h : 1024 * (h + 1)], in_=bank[:].rearrange("p c n -> p (c n)"))
+
+        cs_words = cs_grp[:].bitcast(F32)
+
+        def split(lo, hi, copy):
+            a = lo // 4 if lo < 4 else 1
+            src = cs_raw[a][:, lo - 4 * a : hi - 4 * a, :].rearrange("p i c -> p (i c)").bitcast(F32)
+            copy(
+                out=cs_split[:, lo:hi, :, :],
+                in_=src.rearrange("p (i r u) -> p i u r", u=2, r=P),
+            )
+
+        def turn(i, n, copy):
+            bank = psum.tile([P, 2, 2, P], F32, name="bank")
+            for s in range(n):
+                for u in range(2):
+                    nc.tensor.transpose(bank[:, s, u, :], cs_split[:, i + s, u, :], ident_f[:])
+            copy(
+                out=cs_words[:, P * i : P * (i + n), :].rearrange("p (s r) u -> p s r u", r=P),
+                in_=bank[:, 0:n, :, :].rearrange("p s u r -> p s r u"),
+            )
+
+        split(0, 2, nc.vector.tensor_copy)
+        split(2, 4, nc.vector.tensor_copy)
+        quant(0, 0)
+        turn(0, 2, nc.scalar.copy)
+        turn(2, 2, nc.scalar.copy)
+        split(4, 6, nc.vector.tensor_copy)
+        split(6, 9, nc.vector.tensor_copy)
+        turn(4, 2, nc.vector.tensor_copy)
+        turn(6, 2, nc.scalar.copy)
+        turn(8, 1, nc.vector.tensor_copy)
+
+        def quant_cs(lo, hi):
+            nc.vector.quantize_mx(
+                out=cs_codes[:, lo:hi].bitcast(E4M3), scales=cs_scales[:, lo:hi],
+                in_=cs_grp[:, lo:hi, :].rearrange("p r k -> p (r k)"),
+            )
+
+        for k in range(4):
+            if k > 0:
+                inter(k, 0, COLS_V0 if k < 3 else COLS_V1)
+                lo = 512 * (k - 1)
+                quant_cs(lo, min(lo + 512, T))
+                quant(k, 0)
+            for i in range(8):
+                mm(i, 0, k, k == 0, k == 3)
+
+        inter(0, 1, COLS_V1)
+        epi(0, 0)
+        for k in range(4):
+            mm(8, 0, k, k == 0, k == 3)
+        epi(1, 0)
+        quant(0, 1)
+        inter(1, 1, COLS_V1)
+        epi(2, 0)
+        quant(1, 1)
+        inter(2, 1, COLS_V)
+
+        for b in (1, 2, 3):
+            for t in range(18):
+                step = {4: (2, b), 8: (3, b), 13: (0, b + 1), 17: (1, b + 1)}.get(t)
+                if step and step[1] < 4:
+                    k, c = step
+                    quant(k, c)
+                    nxt = 4 * c + k + 1
+                    if nxt < 16:
+                        inter(nxt % 4, nxt // 4, COLS_V)
+                i = t % 8 if t < 16 else 8
+                first = t < 8 or t == 16
+                k0 = 0 if first else 2
+                mm(i, b, k0, first, False)
+                mm(i, b, k0 + 1, False, not first)
+                if b == 1 and t < 6:
+                    epi(3 + t, 0)
+                if b > 1 and t in (1, 3, 5, 7):
+                    epi(5 + t // 2, b - 1)
+                if b < 3 and t in (9, 11, 13, 15, 17):
+                    epi((t - 9) // 2, b)
+                if b == 3 and t >= 8 and t < 16:
+                    epi(t - 8, b)
+                if t == 17 and b == 3:
+                    epi(8, 3)

@@ -108,8 +108,8 @@ def tile_congested_nodal_prices_e4_kernel(
 
             def part(copy, lo, hi):
                 copy(
-                    out=tile[:, lo:hi, :],
-                    in_=src[:, :, c0 + lo : c0 + hi].rearrange("p j n -> p n j"),
+                    out=tile[:, lo:hi, :].rearrange("p (n i) j -> p n j i", i=4),
+                    in_=src[:, :, c0 + lo : c0 + hi].rearrange("p j (n i) -> p n j i", i=4),
                 )
 
             if v > 0:
@@ -234,25 +234,33 @@ def tile_congested_nodal_prices_e4_kernel(
 
         for b in (1, 2, 3):
             for t in range(18):
-                step = {4: (2, b), 8: (3, b), 13: (0, b + 1), 17: (1, b + 1)}.get(t)
+                step = {6: (2, b), 8: (3, b), 13: (0, b + 1), 17: (1, b + 1)}.get(t)
                 if step and step[1] < 4:
                     k, c = step
                     quant(k, c)
                     nxt = 4 * c + k + 1
                     if nxt < 16:
                         inter(nxt % 4, nxt // 4, COLS_V)
-                i = t % 8 if t < 16 else 8
-                first = t < 8 or t == 16
-                k0 = 0 if first else 2
-                mm(i, b, k0, first, False)
-                mm(i, b, k0 + 1, False, not first)
+                if t < 8:
+                    mm(t, b, 0, True, False)
+                    mm(t, b, 1, False, False)
+                elif t < 16:
+                    k = 2 + (t // 2) % 2
+                    i = 4 * ((t - 8) // 4) + 2 * (t % 2)
+                    mm(i, b, k, False, k == 3)
+                    mm(i + 1, b, k, False, k == 3)
+                else:
+                    k = 2 * (t - 16)
+                    mm(8, b, k, k == 0, False)
+                    mm(8, b, k + 1, False, k == 2)
                 if b == 1 and t < 6:
                     epi(3 + t, 0)
                 if b > 1 and t in (1, 3, 5, 7):
                     epi(5 + t // 2, b - 1)
-                if b < 3 and t in (9, 11, 13, 15, 17):
-                    epi((t - 9) // 2, b)
-                if b == 3 and t >= 8 and t < 16:
-                    epi(t - 8, b)
-                if t == 17 and b == 3:
-                    epi(8, 3)
+                if b < 3 and t in (11, 12, 13, 15, 17):
+                    epi((11, 12, 13, 15, 17).index(t), b)
+                if b == 3 and t in (10, 11, 14, 15):
+                    i = 4 * ((t - 8) // 4) + 2 * (t % 2)
+                    epi(i, b)
+                    epi(i + 1, b)
+        epi(8, 3)

@@ -21,10 +21,9 @@ NB = 512
 NI = T // P
 NG = L // 512
 NBLK = B // NB
-COLS_F = 288
-COLS_V0 = 192
-COLS_V1 = 288
-COLS_V = 64
+ACC_BANKS = (0, 1, 2, 5, 4, 6, 7, 3)
+EARLY = 2
+SH = dict(f=288, a=256, c=192, g=192, p=192, q=192, r=0, s=64, t=64)
 
 
 def tile_congested_nodal_prices_e4_kernel(
@@ -35,7 +34,7 @@ def tile_congested_nodal_prices_e4_kernel(
         keep = ctx.enter_context(tc.tile_pool(name="keep", bufs=1))
         work = ctx.enter_context(tc.tile_pool(name="work", bufs=4))
         res = ctx.enter_context(tc.tile_pool(name="res", bufs=9))
-        psum = ctx.enter_context(tc.psum_pool(name="psum", bufs=8))
+        psum = ctx.enter_context(tc.psum_pool(name="psum", bufs=1))
 
         vec = keep.tile([P, P], BF16, name="vec", align_bytes=64)
         vec_t = keep.tile([P, P], BF16, name="vec_t", align_bytes=64)
@@ -43,7 +42,11 @@ def tile_congested_nodal_prices_e4_kernel(
         ident_f = keep.tile([P, P], F32, name="ident_f", align_bytes=64)
         d_bc = keep.tile([P, B], BF16, name="d_bc", align_bytes=64)
         g_scales = keep.tile([P, NG, T], U8, name="g_scales", align_bytes=64)
-        g_words = [keep.tile([P, T], U32, name="g_words%d" % g, align_bytes=64) for g in range(NG)]
+        g_cut = [((0, 512), (512, T)) if g == 0 else ((0, T),) for g in range(NG)]
+        g_words = [
+            [keep.tile([P, hi - lo], U32, name="g_words%d_%d" % (g, lo), align_bytes=64) for lo, hi in g_cut[g]]
+            for g in range(NG)
+        ]
         cs_raw = [keep.tile([P, n, C], BF16, name="cs_raw%d" % a, align_bytes=64) for a, n in enumerate((4, 5))]
         cs_split = keep.tile([P, NI, 2, P], F32, name="cs_split", align_bytes=64)
         cs_grp = keep.tile([P, T, 4], BF16, name="cs_grp", align_bytes=64)
@@ -66,34 +69,38 @@ def tile_congested_nodal_prices_e4_kernel(
         nc.vector.memset(g_scales[:].rearrange("p g n -> p (g n)").bitcast(I32), 0)
         make_identity(nc, ident_b[:])
         make_identity(nc, ident_f[:])
-        nc.scalar.dma_start(out=vec[0:16, :], in_=delivery.rearrange("(c p) -> c p", p=P))
-        nc.scalar.dma_start(out=vec[16:25, :], in_=energy.rearrange("(c p) -> c p", p=P))
-        for r in range(4):
-            nc.scalar.dma_start(
-                out=g_scales[r:P:32, :, :].bitcast(I32),
-                in_=shadow_scales.rearrange("g (q r) n -> r q g n", r=4)[r].bitcast(I32),
-            )
-
+        energy_rows = energy.rearrange("(c p) -> c p", p=P)
+        nc.sync.dma_start(out=vec[0:16, :], in_=delivery.rearrange("(c p) -> c p", p=P))
+        nc.sync.dma_start(out=vec[16:24, :], in_=energy_rows[0:8, :])
+        nc.sync.dma_start(out=vec[24:25, :], in_=energy_rows[8:9, :])
         def load_rows(k, b):
             src = otdf if k == 3 else ptdf[512 * k : 512 * (k + 1), :]
             c0, n = ((0, 512), (512, 512), (1024, 1024))[b]
             nc.sync.dma_start(out=raw[k, b][:], in_=src.rearrange("(p j) b -> p j b", j=4)[:, :, c0 : c0 + n])
 
-        def load_g(g):
+        def load_g(g, part):
+            lo, hi = g_cut[g][part]
             nc.sync.dma_start(
-                out=g_words[g][:].bitcast(I32),
-                in_=shadow_words[g].rearrange("p n t -> p (n t)").bitcast(I32),
+                out=g_words[g][part][:].bitcast(I32),
+                in_=shadow_words[g].rearrange("p n t -> p (n t)")[:, 4 * lo : 4 * hi].bitcast(I32),
             )
 
         cs_rows = cshadow.rearrange("(i p) c -> p i c", p=P)
         load_rows(0, 0)
         nc.sync.dma_start(out=cs_raw[0][:], in_=cs_rows[:, 0:4, :])
+        load_g(0, 0)
         nc.sync.dma_start(out=cs_raw[1][:], in_=cs_rows[:, 4:9, :])
-        load_g(0)
-        for g in (1, 2):
-            load_rows(g, 0)
-            load_g(g)
+        for r in range(4):
+            nc.scalar.dma_start(
+                out=g_scales[r:P:32, :, :].bitcast(I32),
+                in_=shadow_scales.rearrange("g (q r) n -> r q g n", r=4)[r].bitcast(I32),
+            )
+        load_g(0, 1)
+        load_rows(1, 0)
+        load_g(1, 0)
         load_rows(3, 0)
+        load_rows(2, 0)
+        load_g(2, 0)
         for b in (1, 2):
             for k in range(4):
                 load_rows(k, b)
@@ -127,14 +134,15 @@ def tile_congested_nodal_prices_e4_kernel(
 
         def mm(i, b, k, start, stop):
             if start:
-                bank = psum.tile([P, NB], F32, name="bank")
-                acc[i, b] = bank
+                acc[i, b] = psum.tile([P, NB], F32, name="bank%d" % ACC_BANKS[(9 * b + i) % 8])
             cols = slice(P * i, P * (i + 1))
             if k == 3:
                 lhs = cs_codes[:, cols].bitcast(E4M3)
                 lhs_s = cs_scales[:, cols]
             else:
-                lhs = g_words[k][:, cols].bitcast(E5M2)
+                part = 1 if k == 0 and i > 3 else 0
+                lo = g_cut[k][part][0]
+                lhs = g_words[k][part][:, cols.start - lo : cols.stop - lo].bitcast(E5M2)
                 lhs_s = g_scales[:, k, cols]
             nc.tensor.matmul_mx(
                 out=acc[i, b][:], lhsT=lhs, lhsT_scale=lhs_s,
@@ -164,12 +172,12 @@ def tile_congested_nodal_prices_e4_kernel(
             if b > 1:
                 nc.sync.dma_start(out=out[rows, cols], in_=dst)
 
-        bank = psum.tile([P, P], BF16, name="bank")
+        bank = psum.tile([P, P], BF16, name="bank0")
         nc.tensor.transpose(bank[:], vec[:], ident_b[:])
         nc.vector.tensor_copy(out=vec_t[:], in_=bank[:])
-        inter(0, 0, COLS_F)
+        inter(0, 0, SH['f'])
         for h in range(2):
-            bank = psum.tile([P, 8, P], BF16, name="bank")
+            bank = psum.tile([P, 8, P], BF16, name="bank%d" % (1 + h))
             for c in range(8):
                 col = vec_t[:, 8 * h + c : 8 * h + c + 1]
                 nc.tensor.transpose(bank[:, c, :], col.to_broadcast([P, P]), ident_b[:])
@@ -185,8 +193,8 @@ def tile_congested_nodal_prices_e4_kernel(
                 in_=src.rearrange("p (i r u) -> p i u r", u=2, r=P),
             )
 
-        def turn(i, n, copy):
-            bank = psum.tile([P, 2, 2, P], F32, name="bank")
+        def turn(i, n, where, copy):
+            bank = psum.tile([P, 2, 2, P], F32, name="bank%d" % where)
             for s in range(n):
                 for u in range(2):
                     nc.tensor.transpose(bank[:, s, u, :], cs_split[:, i + s, u, :], ident_f[:])
@@ -195,42 +203,46 @@ def tile_congested_nodal_prices_e4_kernel(
                 in_=bank[:, 0:n, :, :].rearrange("p s u r -> p s r u"),
             )
 
-        split(0, 2, nc.vector.tensor_copy)
-        split(2, 4, nc.vector.tensor_copy)
-        quant(0, 0)
-        turn(0, 2, nc.scalar.copy)
-        turn(2, 2, nc.scalar.copy)
-        split(4, 6, nc.vector.tensor_copy)
-        split(6, 9, nc.vector.tensor_copy)
-        turn(4, 2, nc.vector.tensor_copy)
-        turn(6, 2, nc.scalar.copy)
-        turn(8, 1, nc.vector.tensor_copy)
-
         def quant_cs(lo, hi):
             nc.vector.quantize_mx(
                 out=cs_codes[:, lo:hi].bitcast(E4M3), scales=cs_scales[:, lo:hi],
                 in_=cs_grp[:, lo:hi, :].rearrange("p r k -> p (r k)"),
             )
 
-        for k in range(4):
-            if k > 0:
-                inter(k, 0, COLS_V0 if k < 3 else COLS_V1)
-                lo = 512 * (k - 1)
-                quant_cs(lo, min(lo + 512, T))
-                quant(k, 0)
+        split(0, 2, nc.vector.tensor_copy)
+        split(2, 4, nc.vector.tensor_copy)
+        quant(0, 0)
+        turn(0, 2, 3, nc.scalar.copy)
+        turn(2, 2, 4, nc.scalar.copy)
+        for i in range(EARLY):
+            mm(i, 0, 0, True, False)
+        split(4, 6, nc.vector.tensor_copy)
+        split(6, 9, nc.vector.tensor_copy)
+        turn(4, 2, 6, nc.vector.tensor_copy)
+        turn(6, 2, 7, nc.scalar.copy)
+        turn(8, 1, 3, nc.vector.tensor_copy)
+        for i in range(EARLY, 8):
+            mm(i, 0, 0, True, False)
+        for n, k in enumerate((1, 3, 2)):
+            inter(k, 0, SH['acg'[n]])
+            quant(k, 0)
+            if n == 0:
+                quant_cs(0, 512)
+                quant_cs(512, 1024)
+                quant_cs(1024, 1152)
             for i in range(8):
-                mm(i, 0, k, k == 0, k == 3)
+                mm(i, 0, k, False, k == 2)
 
-        inter(0, 1, COLS_V1)
+        inter(0, 1, SH['p'])
         epi(0, 0)
         for k in range(4):
             mm(8, 0, k, k == 0, k == 3)
         epi(1, 0)
         quant(0, 1)
-        inter(1, 1, COLS_V1)
+        inter(1, 1, SH['q'])
         epi(2, 0)
         quant(1, 1)
-        inter(2, 1, COLS_V)
+        inter(2, 1, SH['r'])
 
         for b in (1, 2, 3):
             for t in range(18):
@@ -240,7 +252,7 @@ def tile_congested_nodal_prices_e4_kernel(
                     quant(k, c)
                     nxt = 4 * c + k + 1
                     if nxt < 16:
-                        inter(nxt % 4, nxt // 4, COLS_V)
+                        inter(nxt % 4, nxt // 4, SH['s'] if nxt < 10 else SH['t'])
                 if t < 8:
                     mm(t, b, 0, True, False)
                     mm(t, b, 1, False, False)

@@ -41,17 +41,17 @@ def tile_congested_nodal_prices_e4_kernel(
         ident_b = keep.tile([P, P], BF16, name="ident_b", align_bytes=64)
         ident_f = keep.tile([P, P], F32, name="ident_f", align_bytes=64)
         d_bc = keep.tile([P, B], BF16, name="d_bc", align_bytes=64)
-        g_scales = keep.tile([P, NG, T], U8, name="g_scales", align_bytes=64)
+        g_scales = keep.tile([P, NG, T], U8, name="g_scales", align_bytes=256)
         g_cut = [((0, 512), (512, T)) if g == 0 else ((0, T),) for g in range(NG)]
         g_words = [
-            [keep.tile([P, hi - lo], U32, name="g_words%d_%d" % (g, lo), align_bytes=64) for lo, hi in g_cut[g]]
+            [keep.tile([P, hi - lo], U32, name="g_words%d_%d" % (g, lo), align_bytes=256) for lo, hi in g_cut[g]]
             for g in range(NG)
         ]
         cs_raw = [keep.tile([P, n, C], BF16, name="cs_raw%d" % a, align_bytes=64) for a, n in enumerate((4, 5))]
         cs_split = keep.tile([P, NI, 2, P], F32, name="cs_split", align_bytes=64)
-        cs_grp = keep.tile([P, T, 4], BF16, name="cs_grp", align_bytes=64)
-        cs_codes = keep.tile([P, T], U32, name="cs_codes", align_bytes=64)
-        cs_scales = keep.tile([P, T], U8, name="cs_scales", align_bytes=64)
+        cs_grp = keep.tile([P, T, 4], BF16, name="cs_grp", align_bytes=256)
+        cs_codes = keep.tile([P, T], U32, name="cs_codes", align_bytes=256)
+        cs_scales = keep.tile([P, T], U8, name="cs_scales", align_bytes=256)
         raw = {}
         for b, n in ((0, 512), (1, 512), (2, 1024)):
             for k in range(4):
@@ -60,8 +60,8 @@ def tile_congested_nodal_prices_e4_kernel(
         scales = {}
         for b in range(NBLK):
             for k in range(4):
-                codes[k, b] = keep.tile([P, NB], U32, name="codes%d_%d" % (k, b), align_bytes=64)
-                scales[k, b] = keep.tile([P, NB], U8, name="scales%d_%d" % (k, b), align_bytes=64)
+                codes[k, b] = keep.tile([P, NB], U32, name="codes%d_%d" % (k, b), align_bytes=256)
+                scales[k, b] = keep.tile([P, NB], U8, name="scales%d_%d" % (k, b), align_bytes=256)
 
         ctx.enter_context(tc.manual_schedule())
 
@@ -108,7 +108,7 @@ def tile_congested_nodal_prices_e4_kernel(
         grp = {}
 
         def inter(k, b, v):
-            tile = work.tile([P, NB, 4], BF16, name="grouped", align_bytes=64)
+            tile = work.tile([P, NB, 4], BF16, name="grouped", align_bytes=256)
             grp[k, b] = tile
             src = raw[k, min(b, 2)]
             c0 = NB if b == 3 else 0
@@ -162,11 +162,21 @@ def tile_congested_nodal_prices_e4_kernel(
             else:
                 single = res.tile([P, NB], F32, name="single", align_bytes=64)
                 dst = single[:]
+            rows = slice(P * i, P * (i + 1))
+            if (i, b) == (NI - 1, NBLK - 1):
+                for lo in range(0, NB, NB // 2):
+                    part = slice(lo, lo + NB // 2)
+                    half = slice(NB * b + lo, NB * b + lo + NB // 2)
+                    nc.vector.scalar_tensor_tensor(
+                        out=dst[:, part], in0=d_bc[:, half], scalar=vec_t[:, 16 + i : 17 + i],
+                        in1=acc[i, b][:, part], op0=MULT, op1=SUB,
+                    )
+                    nc.sync.dma_start(out=out[rows, half], in_=dst[:, part])
+                return
             nc.vector.scalar_tensor_tensor(
                 out=dst, in0=d_bc[:, cols], scalar=vec_t[:, 16 + i : 17 + i],
                 in1=acc[i, b][:], op0=MULT, op1=SUB,
             )
-            rows = slice(P * i, P * (i + 1))
             if b == 1:
                 nc.sync.dma_start(out=out[rows, 0 : 2 * NB], in_=pair[i][:])
             if b > 1:

@@ -22,7 +22,7 @@ NI = T // P
 NG = L // 512
 NBLK = B // NB
 ACC_BANKS = (0, 1, 2, 5, 4, 6, 7, 3)
-EARLY = 2
+PITCH = 256
 SH = dict(f=288, a=256, c=192, g=192, p=192, q=192, r=0, s=64, t=64)
 
 
@@ -41,17 +41,22 @@ def tile_congested_nodal_prices_e4_kernel(
         ident_b = keep.tile([P, P], BF16, name="ident_b", align_bytes=64)
         ident_f = keep.tile([P, P], F32, name="ident_f", align_bytes=64)
         d_bc = keep.tile([P, B], BF16, name="d_bc", align_bytes=64)
-        g_scales = keep.tile([P, NG, T], U8, name="g_scales", align_bytes=256)
+        g_scales = keep.tile([P, NG, T + P], U8, name="g_scales", align_bytes=256)
+        g_odd = keep.tile([P, NG, 4, PITCH], U8, name="g_odd", align_bytes=256)
         g_cut = [((0, 512), (512, T)) if g == 0 else ((0, T),) for g in range(NG)]
         g_words = [
             [keep.tile([P, hi - lo], U32, name="g_words%d_%d" % (g, lo), align_bytes=256) for lo, hi in g_cut[g]]
             for g in range(NG)
         ]
         cs_raw = [keep.tile([P, n, C], BF16, name="cs_raw%d" % a, align_bytes=64) for a, n in enumerate((4, 5))]
-        cs_split = keep.tile([P, NI, 2, P], F32, name="cs_split", align_bytes=64)
+        cs_split = [
+            res.tile([P, 4, 2, P], F32, name="double", align_bytes=64),
+            res.tile([P, 4, 2, P], F32, name="double", align_bytes=64),
+            keep.tile([P, 1, 2, P], F32, name="cs_split_rest", align_bytes=64),
+        ]
         cs_grp = keep.tile([P, T, 4], BF16, name="cs_grp", align_bytes=256)
         cs_codes = keep.tile([P, T], U32, name="cs_codes", align_bytes=256)
-        cs_scales = keep.tile([P, T], U8, name="cs_scales", align_bytes=256)
+        cs_scales = keep.tile([P, NI, PITCH], U8, name="cs_scales", align_bytes=256)
         raw = {}
         for b, n in ((0, 512), (1, 512), (2, 1024)):
             for k in range(4):
@@ -92,7 +97,7 @@ def tile_congested_nodal_prices_e4_kernel(
         nc.sync.dma_start(out=cs_raw[1][:], in_=cs_rows[:, 4:9, :])
         for r in range(4):
             nc.scalar.dma_start(
-                out=g_scales[r:P:32, :, :].bitcast(I32),
+                out=g_scales[r:P:32, :, 0:T].bitcast(I32),
                 in_=shadow_scales.rearrange("g (q r) n -> r q g n", r=4)[r].bitcast(I32),
             )
         load_g(0, 1)
@@ -138,12 +143,12 @@ def tile_congested_nodal_prices_e4_kernel(
             cols = slice(P * i, P * (i + 1))
             if k == 3:
                 lhs = cs_codes[:, cols].bitcast(E4M3)
-                lhs_s = cs_scales[:, cols]
+                lhs_s = cs_scales[:, i, 0:P]
             else:
                 part = 1 if k == 0 and i > 3 else 0
                 lo = g_cut[k][part][0]
                 lhs = g_words[k][part][:, cols.start - lo : cols.stop - lo].bitcast(E5M2)
-                lhs_s = g_scales[:, k, cols]
+                lhs_s = g_odd[:, k, i // 2, 0:P] if i % 2 else g_scales[:, k, cols]
             nc.tensor.matmul_mx(
                 out=acc[i, b][:], lhsT=lhs, lhsT_scale=lhs_s,
                 rhs=codes[k, b][:].bitcast(E4M3), rhs_scale=scales[k, b][:],
@@ -199,7 +204,7 @@ def tile_congested_nodal_prices_e4_kernel(
             a = lo // 4 if lo < 4 else 1
             src = cs_raw[a][:, lo - 4 * a : hi - 4 * a, :].rearrange("p i c -> p (i c)").bitcast(F32)
             copy(
-                out=cs_split[:, lo:hi, :, :],
+                out=cs_split[lo // 4][:, lo % 4 : lo % 4 + hi - lo, :, :],
                 in_=src.rearrange("p (i r u) -> p i u r", u=2, r=P),
             )
 
@@ -207,37 +212,44 @@ def tile_congested_nodal_prices_e4_kernel(
             bank = psum.tile([P, 2, 2, P], F32, name="bank%d" % where)
             for s in range(n):
                 for u in range(2):
-                    nc.tensor.transpose(bank[:, s, u, :], cs_split[:, i + s, u, :], ident_f[:])
+                    nc.tensor.transpose(bank[:, s, u, :], cs_split[(i + s) // 4][:, (i + s) % 4, u, :], ident_f[:])
             copy(
                 out=cs_words[:, P * i : P * (i + n), :].rearrange("p (s r) u -> p s r u", r=P),
                 in_=bank[:, 0:n, :, :].rearrange("p s u r -> p s r u"),
             )
 
         def quant_cs(lo, hi):
-            nc.vector.quantize_mx(
-                out=cs_codes[:, lo:hi].bitcast(E4M3), scales=cs_scales[:, lo:hi],
-                in_=cs_grp[:, lo:hi, :].rearrange("p r k -> p (r k)"),
-            )
+            for i in range(lo // P, hi // P):
+                rows = slice(P * i, P * (i + 1))
+                nc.vector.quantize_mx(
+                    out=cs_codes[:, rows].bitcast(E4M3), scales=cs_scales[:, i, 0:P],
+                    in_=cs_grp[:, rows, :].rearrange("p r k -> p (r k)"),
+                )
 
         split(0, 2, nc.vector.tensor_copy)
         split(2, 4, nc.vector.tensor_copy)
         quant(0, 0)
         turn(0, 2, 3, nc.scalar.copy)
         turn(2, 2, 4, nc.scalar.copy)
-        for i in range(EARLY):
+        for i in (0, 2):
             mm(i, 0, 0, True, False)
         split(4, 6, nc.vector.tensor_copy)
-        split(6, 9, nc.vector.tensor_copy)
+        split(6, 8, nc.vector.tensor_copy)
+        split(8, 9, nc.vector.tensor_copy)
+        nc.vector.tensor_copy(
+            out=g_odd[:, :, :, 0:P].bitcast(I32),
+            in_=g_scales[:].rearrange("p g (i two n) -> p g i two n", two=2, n=P)[:, :, 0:4, 1, :].bitcast(I32),
+        )
+        quant_cs(0, 512)
         turn(4, 2, 6, nc.vector.tensor_copy)
         turn(6, 2, 7, nc.scalar.copy)
         turn(8, 1, 3, nc.vector.tensor_copy)
-        for i in range(EARLY, 8):
+        for i in (1, 3, 4, 5, 6, 7):
             mm(i, 0, 0, True, False)
         for n, k in enumerate((1, 3, 2)):
             inter(k, 0, SH['acg'[n]])
             quant(k, 0)
             if n == 0:
-                quant_cs(0, 512)
                 quant_cs(512, 1024)
                 quant_cs(1024, 1152)
             for i in range(8):

from contextlib import ExitStack

import concourse.mybir as mybir
from concourse.masks import make_identity

T, L, C, B = 1152, 1536, 512, 2048
FLOPS = 2 * T * B * (L + C)

F32 = mybir.dt.float32
BF16 = mybir.dt.bfloat16
U32 = mybir.dt.uint32
I32 = mybir.dt.int32
U8 = mybir.dt.uint8
E4M3 = mybir.dt.float8_e4m3fn_x4
E5M2 = mybir.dt.float8_e5m2_x4
MULT = mybir.AluOpType.mult
SUB = mybir.AluOpType.subtract

P = 128
NB = 512
NI = T // P
NG = L // 512
NBLK = B // NB
ACC_BANKS = (0, 1, 2, 5, 4, 6, 7, 3)
PITCH = 256
SH = dict(f=288, a=256, c=192, g=192, p=192, q=192, r=0, s=64, t=64)


def tile_congested_nodal_prices_e4_kernel(
    tc, shadow_words, shadow_scales, ptdf, cshadow, otdf, energy, delivery, out
):
    nc = tc.nc
    with ExitStack() as ctx:
        keep = ctx.enter_context(tc.tile_pool(name="keep", bufs=1))
        work = ctx.enter_context(tc.tile_pool(name="work", bufs=4))
        res = ctx.enter_context(tc.tile_pool(name="res", bufs=9))
        psum = ctx.enter_context(tc.psum_pool(name="psum", bufs=1))

        vec = keep.tile([P, P], BF16, name="vec", align_bytes=64)
        vec_t = keep.tile([P, P], BF16, name="vec_t", align_bytes=64)
        ident_b = keep.tile([P, P], BF16, name="ident_b", align_bytes=64)
        ident_f = keep.tile([P, P], F32, name="ident_f", align_bytes=64)
        d_bc = keep.tile([P, B], BF16, name="d_bc", align_bytes=64)
        g_scales = keep.tile([P, NG, T + P], U8, name="g_scales", align_bytes=256)
        g_odd = keep.tile([P, NG, 4, PITCH], U8, name="g_odd", align_bytes=256)
        g_cut = [((0, 512), (512, T)) if g == 0 else ((0, T),) for g in range(NG)]
        g_words = [
            [keep.tile([P, hi - lo], U32, name="g_words%d_%d" % (g, lo), align_bytes=256) for lo, hi in g_cut[g]]
            for g in range(NG)
        ]
        cs_raw = [keep.tile([P, n, C], BF16, name="cs_raw%d" % a, align_bytes=64) for a, n in enumerate((4, 5))]
        cs_split = [
            res.tile([P, 4, 2, P], F32, name="double", align_bytes=64),
            res.tile([P, 4, 2, P], F32, name="double", align_bytes=64),
            keep.tile([P, 1, 2, P], F32, name="cs_split_rest", align_bytes=64),
        ]
        cs_grp = keep.tile([P, T, 4], BF16, name="cs_grp", align_bytes=256)
        cs_codes = keep.tile([P, T], U32, name="cs_codes", align_bytes=256)
        cs_scales = keep.tile([P, NI, PITCH], U8, name="cs_scales", align_bytes=256)
        raw = {}
        for b, n in ((0, 512), (1, 512), (2, 1024)):
            for k in range(4):
                raw[k, b] = keep.tile([P, 4, n], BF16, name="raw%d_%d" % (k, b), align_bytes=64)
        codes = {}
        scales = {}
        for b in range(NBLK):
            for k in range(4):
                codes[k, b] = keep.tile([P, NB], U32, name="codes%d_%d" % (k, b), align_bytes=256)
                scales[k, b] = keep.tile([P, NB], U8, name="scales%d_%d" % (k, b), align_bytes=256)

        ctx.enter_context(tc.manual_schedule())

        nc.vector.memset(vec[:], 0.0)
        nc.vector.memset(g_scales[:].rearrange("p g n -> p (g n)").bitcast(I32), 0)
        make_identity(nc, ident_b[:])
        make_identity(nc, ident_f[:])
        energy_rows = energy.rearrange("(c p) -> c p", p=P)
        nc.sync.dma_start(out=vec[0:16, :], in_=delivery.rearrange("(c p) -> c p", p=P))
        nc.sync.dma_start(out=vec[16:24, :], in_=energy_rows[0:8, :])
        nc.sync.dma_start(out=vec[24:25, :], in_=energy_rows[8:9, :])
        def load_rows(k, b):
            src = otdf if k == 3 else ptdf[512 * k : 512 * (k + 1), :]
            c0, n = ((0, 512), (512, 512), (1024, 1024))[b]
            nc.sync.dma_start(out=raw[k, b][:], in_=src.rearrange("(p j) b -> p j b", j=4)[:, :, c0 : c0 + n])

        def load_g(g, part):
            lo, hi = g_cut[g][part]
            nc.sync.dma_start(
                out=g_words[g][part][:].bitcast(I32),
                in_=shadow_words[g].rearrange("p n t -> p (n t)")[:, 4 * lo : 4 * hi].bitcast(I32),
            )

        cs_rows = cshadow.rearrange("(i p) c -> p i c", p=P)
        load_rows(0, 0)
        nc.sync.dma_start(out=cs_raw[0][:], in_=cs_rows[:, 0:4, :])
        load_g(0, 0)
        nc.sync.dma_start(out=cs_raw[1][:], in_=cs_rows[:, 4:9, :])
        for r in range(4):
            nc.scalar.dma_start(
                out=g_scales[r:P:32, :, 0:T].bitcast(I32),
                in_=shadow_scales.rearrange("g (q r) n -> r q g n", r=4)[r].bitcast(I32),
            )
        load_g(0, 1)
        load_rows(1, 0)
        load_g(1, 0)
        load_rows(3, 0)
        load_rows(2, 0)
        load_g(2, 0)
        for b in (1, 2):
            for k in range(4):
                load_rows(k, b)

        grp = {}

        def inter(k, b, v):
            tile = work.tile([P, NB, 4], BF16, name="grouped", align_bytes=256)
            grp[k, b] = tile
            src = raw[k, min(b, 2)]
            c0 = NB if b == 3 else 0

            def part(copy, lo, hi):
                copy(
                    out=tile[:, lo:hi, :].rearrange("p (n i) j -> p n j i", i=4),
                    in_=src[:, :, c0 + lo : c0 + hi].rearrange("p j (n i) -> p n j i", i=4),
                )

            if v > 0:
                part(nc.vector.tensor_copy, 0, v)
            part(nc.scalar.copy, v, NB)

        def quant(k, b):
            nc.vector.quantize_mx(
                out=codes[k, b][:].bitcast(E4M3),
                scales=scales[k, b][:],
                in_=grp[k, b][:].rearrange("p n j -> p (n j)"),
            )

        acc = {}

        def mm(i, b, k, start, stop):
            if start:
                acc[i, b] = psum.tile([P, NB], F32, name="bank%d" % ACC_BANKS[(9 * b + i) % 8])
            cols = slice(P * i, P * (i + 1))
            if k == 3:
                lhs = cs_codes[:, cols].bitcast(E4M3)
                lhs_s = cs_scales[:, i, 0:P]
            else:
                part = 1 if k == 0 and i > 3 else 0
                lo = g_cut[k][part][0]
                lhs = g_words[k][part][:, cols.start - lo : cols.stop - lo].bitcast(E5M2)
                lhs_s = g_odd[:, k, i // 2, 0:P] if i % 2 else g_scales[:, k, cols]
            nc.tensor.matmul_mx(
                out=acc[i, b][:], lhsT=lhs, lhsT_scale=lhs_s,
                rhs=codes[k, b][:].bitcast(E4M3), rhs_scale=scales[k, b][:],
                start=start, stop=stop,
            )

        pair = {}

        def epi(i, b):
            cols = slice(NB * b, NB * (b + 1))
            if b < 2:
                if b == 0:
                    double = res.tile([P, 2 * NB], F32, name="double", align_bytes=64)
                    pair[i] = double
                dst = pair[i][:, NB * b : NB * (b + 1)]
            else:
                single = res.tile([P, NB], F32, name="single", align_bytes=64)
                dst = single[:]
            rows = slice(P * i, P * (i + 1))
            if (i, b) == (NI - 1, NBLK - 1):
                for lo in range(0, NB, NB // 2):
                    part = slice(lo, lo + NB // 2)
                    half = slice(NB * b + lo, NB * b + lo + NB // 2)
                    nc.vector.scalar_tensor_tensor(
                        out=dst[:, part], in0=d_bc[:, half], scalar=vec_t[:, 16 + i : 17 + i],
                        in1=acc[i, b][:, part], op0=MULT, op1=SUB,
                    )
                    nc.sync.dma_start(out=out[rows, half], in_=dst[:, part])
                return
            nc.vector.scalar_tensor_tensor(
                out=dst, in0=d_bc[:, cols], scalar=vec_t[:, 16 + i : 17 + i],
                in1=acc[i, b][:], op0=MULT, op1=SUB,
            )
            if b == 1:
                nc.sync.dma_start(out=out[rows, 0 : 2 * NB], in_=pair[i][:])
            if b > 1:
                nc.sync.dma_start(out=out[rows, cols], in_=dst)

        bank = psum.tile([P, P], BF16, name="bank0")
        nc.tensor.transpose(bank[:], vec[:], ident_b[:])
        nc.vector.tensor_copy(out=vec_t[:], in_=bank[:])
        inter(0, 0, SH['f'])
        for h in range(2):
            bank = psum.tile([P, 8, P], BF16, name="bank%d" % (1 + h))
            for c in range(8):
                col = vec_t[:, 8 * h + c : 8 * h + c + 1]
                nc.tensor.transpose(bank[:, c, :], col.to_broadcast([P, P]), ident_b[:])
            nc.scalar.copy(out=d_bc[:, 1024 * h : 1024 * (h + 1)], in_=bank[:].rearrange("p c n -> p (c n)"))

        cs_words = cs_grp[:].bitcast(F32)

        def split(lo, hi, copy):
            a = lo // 4 if lo < 4 else 1
            src = cs_raw[a][:, lo - 4 * a : hi - 4 * a, :].rearrange("p i c -> p (i c)").bitcast(F32)
            copy(
                out=cs_split[lo // 4][:, lo % 4 : lo % 4 + hi - lo, :, :],
                in_=src.rearrange("p (i r u) -> p i u r", u=2, r=P),
            )

        def turn(i, n, where, copy):
            bank = psum.tile([P, 2, 2, P], F32, name="bank%d" % where)
            for s in range(n):
                for u in range(2):
                    nc.tensor.transpose(bank[:, s, u, :], cs_split[(i + s) // 4][:, (i + s) % 4, u, :], ident_f[:])
            copy(
                out=cs_words[:, P * i : P * (i + n), :].rearrange("p (s r) u -> p s r u", r=P),
                in_=bank[:, 0:n, :, :].rearrange("p s u r -> p s r u"),
            )

        def quant_cs(lo, hi):
            for i in range(lo // P, hi // P):
                rows = slice(P * i, P * (i + 1))
                nc.vector.quantize_mx(
                    out=cs_codes[:, rows].bitcast(E4M3), scales=cs_scales[:, i, 0:P],
                    in_=cs_grp[:, rows, :].rearrange("p r k -> p (r k)"),
                )

        split(0, 2, nc.vector.tensor_copy)
        split(2, 4, nc.vector.tensor_copy)
        quant(0, 0)
        turn(0, 2, 3, nc.scalar.copy)
        turn(2, 2, 4, nc.scalar.copy)
        for i in (0, 2):
            mm(i, 0, 0, True, False)
        split(4, 6, nc.vector.tensor_copy)
        split(6, 8, nc.vector.tensor_copy)
        split(8, 9, nc.vector.tensor_copy)
        nc.vector.tensor_copy(
            out=g_odd[:, :, :, 0:P].bitcast(I32),
            in_=g_scales[:].rearrange("p g (i two n) -> p g i two n", two=2, n=P)[:, :, 0:4, 1, :].bitcast(I32),
        )
        quant_cs(0, 512)
        turn(4, 2, 6, nc.vector.tensor_copy)
        turn(6, 2, 7, nc.scalar.copy)
        turn(8, 1, 3, nc.vector.tensor_copy)
        for i in (1, 3, 4, 5, 6, 7):
            mm(i, 0, 0, True, False)
        for n, k in enumerate((1, 3, 2)):
            inter(k, 0, SH['acg'[n]])
            quant(k, 0)
            if n == 0:
                quant_cs(512, 1024)
                quant_cs(1024, 1152)
            for i in range(8):
                mm(i, 0, k, False, k == 2)

        inter(0, 1, SH['p'])
        epi(0, 0)
        for k in range(4):
            mm(8, 0, k, k == 0, k == 3)
        epi(1, 0)
        quant(0, 1)
        inter(1, 1, SH['q'])
        epi(2, 0)
        quant(1, 1)
        inter(2, 1, SH['r'])

        for b in (1, 2, 3):
            for t in range(18):
                step = {6: (2, b), 8: (3, b), 13: (0, b + 1), 17: (1, b + 1)}.get(t)
                if step and step[1] < 4:
                    k, c = step
                    quant(k, c)
                    nxt = 4 * c + k + 1
                    if nxt < 16:
                        inter(nxt % 4, nxt // 4, SH['s'] if nxt < 10 else SH['t'])
                if t < 8:
                    mm(t, b, 0, True, False)
                    mm(t, b, 1, False, False)
                elif t < 16:
                    k = 2 + (t // 2) % 2
                    i = 4 * ((t - 8) // 4) + 2 * (t % 2)
                    mm(i, b, k, False, k == 3)
                    mm(i + 1, b, k, False, k == 3)
                else:
                    k = 2 * (t - 16)
                    mm(8, b, k, k == 0, False)
                    mm(8, b, k + 1, False, k == 2)
                if b == 1 and t < 6:
                    epi(3 + t, 0)
                if b > 1 and t in (1, 3, 5, 7):
                    epi(5 + t // 2, b - 1)
                if b < 3 and t in (11, 12, 13, 15, 17):
                    epi((11, 12, 13, 15, 17).index(t), b)
                if b == 3 and t in (10, 11, 14, 15):
                    i = 4 * ((t - 8) // 4) + 2 * (t % 2)
                    epi(i, b)
                    epi(i + 1, b)
        epi(8, 3)
